import numpy as np, ml_dtypes
CORES = [12,28,60,100,156,228]
N = 6
import mx_ref
NC = 128
BF = ml_dtypes.bfloat16
def cut(t, i, w=512):
    return t[:, w * i:w * i + w]
def tile(rs):
    return np.stack(rs, axis=2).reshape(128, -1).astype(BF)
def onehot(t, r):
    own, p, b = t[:, :NC], t[:, NC:2 * NC], t[:, 2 * NC:]
    return tile([((own == r) & (p == np.arange(128)[:, None]) & (b == f)).astype(np.float32) for f in range(4)])
def setup_inputs(rng):
    def f(*shape):
        return mx_ref.flush((rng.standard_normal(shape, dtype=np.float32) * np.exp2(rng.integers(-2, 3, shape[:-1] + (1,)))).astype(BF))
    t = np.concatenate([rng.integers(0, N, (N, 1, NC)), rng.integers(0, 128, (N, 1, NC)), rng.integers(0, 4, (N, 1, NC))], axis=2)
    return {"tg": np.broadcast_to(t, (N, 128, 3 * NC)).astype(BF).copy(), "tab": f(N, 128, 4 * 512), "w": f(N, 128, 512)}
def setup_inputs_blocks(rng):
    d = setup_inputs(rng)
    for k in ("tab", "w"): d[k] = mx_ref.spread(d[k], rng, 4)
    return d
def setup_inputs_wide(rng):
    d = setup_inputs(rng)
    for k in ("tab", "w"): d[k] = mx_ref.flush((d[k].astype(np.float32) * np.exp2(rng.integers(-6, 7, (N, 1, 1))).astype(np.float32)).astype(BF))
    return d
def setup_inputs_hot(rng):
    d = setup_inputs(rng); t = d["tg"].astype(np.float32); t[:, :, :NC] = rng.integers(0, N); t[:, :, NC:2 * NC] = np.broadcast_to(rng.integers(0, 4, (N, 1, NC)), (N, 128, NC))
    d["tg"] = t.astype(BF)
    return d
def reference(tg, tab, w):
    y = np.zeros((N, 128, NC), np.float32)
    for j in range(N):
        qw = mx_ref.quantize(w[j])
        for r in range(N):
            o = mx_ref.quantize(onehot(tg[j].astype(np.float32), r))
            e = mx_ref.quantize(tile([mx_ref.matmul(mx_ref.quantize(cut(tab[r], f)), o) for f in range(4)]))
            p = mx_ref.matmul(qw, e)
            y[j] = p if r == 0 else y[j] + p
    return {"y": y}

@@ -1,0 +1,348 @@
+import math
+from concourse.bass import DstId, RemoteDMATransfer
+from concourse.mybir import dt, AluOpType, ActivationFunctionType
+
+Op = AluOpType
+Act = ActivationFunctionType
+NR = 6
+NC = 128
+NBANK = 7
+LN2 = math.log(2.0)
+
+SCRATCH = {
+    "TG": ("sbuf", [128, 384], "bfloat16"),
+    "TGT": ("sbuf", [128, 384], "bfloat16"),
+    "TAB": ("sbuf", [128, 2048], "bfloat16"),
+    "WB": ("sbuf", [128, 512], "bfloat16"),
+    "TC": ("sbuf", [128, 512], "float8_e4m3fn_x4"),
+    "TS": ("sbuf", [128, 512], "uint8"),
+    "WC": ("sbuf", [128, 128], "float8_e4m3fn_x4"),
+    "WS": ("sbuf", [128, 128], "uint8"),
+    "IOT": ("sbuf", [128, 32], "bfloat16"),
+    "KC": ("sbuf", [128, 1], "float32"),
+    "KR": ("sbuf", [128, 1], "float32"),
+    "TBL": ("sbuf", [128, 4, 32], "bfloat16"),
+    "TBP": ("sbuf", [128, 4, 32], "bfloat16"),
+    "E1": ("sbuf", [128, 4], "bfloat16"),
+    "E2": ("sbuf", [128, 4], "bfloat16"),
+    "P1": ("sbuf", [128, 4], "bfloat16"),
+    "X": ("sbuf", [128, 4], "bfloat16"),
+    "MSG": ("sbuf", [128, 4], "bfloat16"),
+    "LAND": ("sbuf", [128, 4 * NR], "bfloat16"),
+    "LANDH": ("sbuf", [128, 4], "bfloat16"),
+    "Y3": ("sbuf", [128, 4, NR * NC], "bfloat16"),
+    "O": ("sbuf", [128, NR * 512], "bfloat16"),
+    "OC": ("sbuf", [128, NR * NC], "float8_e4m3fn_x4"),
+    "OS": ("sbuf", [128, NR * NC], "uint8"),
+    "ROC": ("sbuf", [128, NC], "float8_e4m3fn_x4"),
+    "ROS": ("sbuf", [128, NC], "uint8"),
+    "ET": ("sbuf", [128, NR * 512], "bfloat16"),
+    "EC": ("sbuf", [128, NR * NC], "float8_e4m3fn_x4"),
+    "ES": ("sbuf", [128, NR * NC], "uint8"),
+    "LC": ("sbuf", [128, NR * NC], "float8_e4m3fn_x4"),
+    "LS": ("sbuf", [128, NR * NC], "uint8"),
+    "HC": ("sbuf", [128, 3 * NC], "float8_e4m3fn_x4"),
+    "HS": ("sbuf", [128, 3 * NC], "uint8"),
+    "YS": ("sbuf", [128, NC], "float32"),
+    "ZP": ("psum", [128, 512 * NBANK], "float32"),
+    "YP": ("psum", [128, 512], "float32"),
+}
+NEV = 90
+SEMAPHORES = (["v%d" % i for i in range(NEV)] + ["id%d" % i for i in range(NR)] + ["ee%d" % i for i in range(NR)]
+              + ["hc%d" % i for i in range(3)] + ["hs%d" % i for i in range(3)] + ["idh", "oa", "loc"])
+
+
+def lanes(mask):
+    return [e for e in range(mask.bit_length()) if (mask >> e) & 1]
+
+
+def pack(es):
+    return sum(1 << e for e in es)
+
+
+def split(es, k):
+    n = len(es)
+    if k == 1:
+        return [es]
+    if k == 2:
+        return [es[:n // 2], es[n // 2:]]
+    q = [es[n // 4 * i:n // 4 * (i + 1)] for i in range(4)]
+    return [q[0], q[1], q[2] + q[3]] if k == 3 else q
+
+
+def road(r, T, topo):
+    cores = T.cores
+    me = cores[r]
+    group = [j for j in range(NR) if j == r or topo.same_plane(me, cores[j])]
+    far = [j for j in range(NR) if j not in group]
+    m = len(group)
+    idx = group.index(r)
+    near = [group[(idx + 1 + i) % m] for i in range(m - 1)]
+    chip = [c for c in range(max(0, me - 8), me + 9) if topo.host(c) == topo.host(me) and topo.chip(c) == topo.chip(me) and c != me]
+    port = [c for c in chip if all(topo.may_write(c, cores[j]) for j in far)]
+    h0 = [c for c in port if topo.die(c) == topo.die(me)][0]
+    h1 = [c for c in port if topo.die(c) != topo.die(me)][0]
+    half = len(far) // 2
+    a, b = far[:half], far[half:]
+    if idx % 2:
+        a, b = b, a
+    on = lanes(topo.mask(me, h0))
+    off = lanes(topo.mask(me, cores[near[0]]))
+    up = [e for e in on if e not in off]
+    return {"me": me, "group": group, "far": far, "near": near, "h0": h0, "h1": h1, "pairs": list(zip(a, b)),
+            "on": on, "off": off, "up": up, "big": len(near) > 1}
+
+
+def send(g, T, topo, src, items):
+    tr = []
+    n = 0
+    for d, s, o, sem, es in items:
+        rid, pid = topo.addr(d, src)
+        tr.append(RemoteDMATransfer(dst_ids=[DstId(rid=rid, pnc=pid)], dma_engine_mask=pack(es), remote_sem=sem, src=s, dst=o))
+        n += len(es)
+    g.remote_dma_fused(tr, local_sem=T.sem.loc)
+    return n
+
+
+def cd(t, i, n=1):
+    return t[:, NC * i:NC * (i + n)].bitcast(dt.uint8)
+
+
+def sc(t, i, n=1):
+    return t[:, NC * i:NC * (i + n)]
+
+
+def helper_program(g, core, r, R, T, topo):
+    cores = T.cores
+    first = core == R["h0"]
+    loc = 0
+    if first:
+        g.wait_ge(T.sem.idh, len(R["up"]))
+        parts = split(R["off"], len(R["far"]))
+        loc += send(g, T, topo, core, [(cores[j], T.LANDH[:], T.LAND[:, 4 * r:4 * r + 4], T.sem["id%d" % r], parts[i])
+                                       for i, j in enumerate(R["far"])])
+    todo = []
+    if not first:
+        if R["big"]:
+            todo.append((0, len(R["up"]), R["near"][0], (T.LC, T.LS, r), T.sem["ee%d" % r]))
+        else:
+            todo.append((0, len(R["on"]), R["near"][0], (T.ROC, T.ROS, 0), T.sem.oa))
+    for s, pr in enumerate(R["pairs"]):
+        todo.append((s + 1, len(R["up"] if first else R["off"]), pr[0 if first else 1], (T.LC, T.LS, r), T.sem["ee%d" % r]))
+    for slot, n, j, (bc, bs, at), sem in todo:
+        g.wait_ge(T.sem["hc%d" % slot], n)
+        loc += send(g, T, topo, core, [(cores[j], cd(T.HC, slot), cd(bc, at), sem, R["off"])])
+        g.wait_ge(T.sem["hs%d" % slot], n)
+        loc += send(g, T, topo, core, [(cores[j], sc(T.HS, slot), sc(bs, at), sem, R["off"])])
+    g.wait_ge(T.sem.loc, loc)
+
+
+def rank_core(g, core, r, R, T, topo):
+    cores = T.cores
+    V, S, P = g.vector, g.scalar, g.tensor
+    cnt = [0]
+
+    def ev():
+        cnt[0] += 1
+        return T.sem["v%d" % (cnt[0] - 1)]
+
+    near, far, big = R["near"], R["far"], R["big"]
+    on, off, up = R["on"], R["off"], R["up"]
+    roads = [road(j, T, topo) for j in range(NR)]
+
+    def id_count(j):
+        if j in near:
+            k = roads[j]["near"].index(r)
+            return len(split(roads[j]["off"], len(roads[j]["near"]))[k])
+        k = roads[j]["far"].index(r)
+        return len(split(roads[j]["off"], len(roads[j]["far"]))[k])
+
+    def e_count(j):
+        Q = roads[j]
+        if j in near and Q["big"] and Q["near"].index(r) > 0:
+            return 2 * len(split(Q["off"], 2)[0])
+        return 2 * len(Q["off"])
+
+    s_tg, s_tab, s_w = ev(), ev(), ev()
+    g.sync.dma_start(T.TG[:], T.tg[:]).then_inc(s_tg, 16)
+    g.sync.dma_start(T.TAB[:], T.tab[:]).then_inc(s_tab, 16)
+    g.sync.dma_start(T.WB[:], T.w[:]).then_inc(s_w, 16)
+
+    s_io = ev()
+    for a in range(4):
+        g.iota(T.IOT[32 * a:32 * a + 32, :], [[1, 32]], 32 * a + 1, 0, allow_small_or_imprecise_dtypes=True).then_inc(s_io, 1)
+
+    s_kc, s_kr = ev(), ev()
+    V.memset(T.KC[:], float(r)).then_inc(s_kc, 1)
+    S.wait_ge(s_kc, 1)
+    S.activation(T.KR[:], T.KC[:], Act.Exp, bias=-95.0 * LN2, scale=32.0 * LN2).then_inc(s_kr, 1)
+
+    s_t, s_e, s_p, s_x, s_msg = ev(), ev(), ev(), ev(), ev()
+    V.wait_ge(s_tg, 16)
+    V.transpose(T.TGT[:], T.TG[:]).then_inc(s_t, 1)
+    S.wait_ge(s_t, 1)
+    S.activation(T.E2[:], T.TGT[:, 256:384:32], Act.Exp, scale=8.0 * LN2).then_inc(s_e, 1)
+    S.activation(T.E1[:], T.TGT[:, 0:128:32], Act.Exp, bias=-95.0 * LN2, scale=32.0 * LN2).then_inc(s_e, 1)
+    V.wait_ge(s_t, 1)
+    V.tensor_scalar(T.P1[:], T.TGT[:, 128:256:32], 1.0, None, Op.add).then_inc(s_p, 1)
+    V.wait_ge(s_p, 1)
+    V.wait_ge(s_e, 2)
+    V.tensor_tensor(T.X[:], T.P1[:], T.E2[:], Op.mult).then_inc(s_x, 1)
+    V.wait_ge(s_x, 1)
+    V.tensor_tensor(T.MSG[:], T.X[:], T.E1[:], Op.mult).then_inc(s_msg, 1)
+
+    loc = 0
+    g.wait_ge(s_msg, 1)
+    loc += send(g, T, topo, core, [(R["h0"], T.MSG[:], T.LANDH[:], T.sem.idh, up)])
+    if big:
+        parts = split(off, len(near))
+        loc += send(g, T, topo, core, [(cores[j], T.MSG[:], T.LAND[:, 4 * r:4 * r + 4], T.sem["id%d" % r], parts[i])
+                                       for i, j in enumerate(near)])
+
+    V.wait_ge(s_io, 4)
+    V.wait_ge(s_kr, 1)
+    s_tb = ev()
+    for b in range(4):
+        V.tensor_scalar(T.TBL[:, b, :], T.IOT[:], float(2.0 ** (8 * b)), T.KR[:], Op.mult, Op.mult).then_inc(s_tb, 1)
+    if not big:
+        s_tp = ev()
+        for b in range(4):
+            V.tensor_scalar(T.TBP[:, b, :], T.IOT[:], float(2.0 ** (8 * b + 32 * (near[0] - r))), T.KR[:], Op.mult, Op.mult).then_inc(s_tp, 1)
+
+    def make_o(t0, tab, srcs):
+        n = len(srcs)
+        s_y, s_o, s_q = ev(), ev(), ev()
+        for i, (buf, c0, waits) in enumerate(srcs):
+            for sem, val in waits:
+                V.wait_ge(sem, val)
+            for k in range(4):
+                at = NC * (t0 + i) + 32 * k
+                V.tensor_scalar(T.Y3[:, :, at:at + 32], tab[:], buf[:, c0 + k:c0 + k + 1], None, Op.is_equal).then_inc(s_y, 1)
+        V.wait_ge(s_y, 4 * n)
+        for b in range(4):
+            V.transpose(T.O[:, 512 * t0 + b:512 * (t0 + n):4], T.Y3[:, b, NC * t0:NC * (t0 + n)]).then_inc(s_o, 1)
+        V.wait_ge(s_o, 4)
+        V.quantize_mx(sc(T.OC, t0, n), sc(T.OS, t0, n), T.O[:, 512 * t0:512 * (t0 + n)]).then_inc(s_q, 1)
+        return s_q
+
+    bank = [0]
+    busy = {}
+
+    def mm_z(n, oc, os_, waits):
+        s_c = ev()
+        mine = "v%d" % (cnt[0] - 1)
+        res = []
+        for sem, val in waits:
+            P.wait_ge(sem, val)
+        seen = []
+        for f in range(4):
+            k = bank[0] % NBANK
+            bank[0] += 1
+            if k in busy and busy[k] not in seen:
+                P.wait_ge(T.sem[busy[k]], 4)
+                seen.append(busy[k])
+            busy[k] = mine
+            s_z = ev()
+            P.matmul_mx(T.ZP[:, 512 * k:512 * k + NC * n], sc(T.TC, f), sc(T.TS, f), oc, os_, True, True).then_inc(s_z, 1)
+            res.append((k, s_z))
+        return res, s_c
+
+    def make_e(t0, n, res, s_c):
+        s_q = ev()
+        for f, (k, s_z) in enumerate(res):
+            src = T.ZP[:, 512 * k:512 * k + NC * n]
+            out = T.ET[:, 512 * t0 + f:512 * (t0 + n):4]
+            if f % 2:
+                S.wait_ge(s_z, 1)
+                S.activation(out, src, Act.Copy).then_inc(s_c, 1)
+            else:
+                V.wait_ge(s_z, 1)
+                V.tensor_copy(out, src).then_inc(s_c, 1)
+        V.wait_ge(s_c, 4)
+        V.quantize_mx(sc(T.EC, t0, n), sc(T.ES, t0, n), T.ET[:, 512 * t0:512 * (t0 + n)]).then_inc(s_q, 1)
+        return s_q
+
+    def land(j):
+        return (T.LAND, 4 * j, [(T.sem["id%d" % j], id_count(j))])
+
+    def ship(s_q, items):
+        g.wait_ge(s_q, 1)
+        a = send(g, T, topo, core, [(d, cd(T.EC, t), cd(bc, at), s1, es) for d, t, bc, bs, at, s1, s2, es in items])
+        return a + send(g, T, topo, core, [(d, sc(T.ES, t), sc(bs, at), s2, es) for d, t, bc, bs, at, s1, s2, es in items])
+
+    def via(h, t, slot, es):
+        return (h, t, T.HC, T.HS, slot, T.sem["hc%d" % slot], T.sem["hs%d" % slot], es)
+
+    def straight(j, t, es):
+        sem = T.sem["ee%d" % r]
+        return (cores[j], t, T.LC, T.LS, r, sem, sem, es)
+
+    V.wait_ge(s_tb, 4)
+    if not big:
+        V.wait_ge(s_tp, 4)
+        s_op = make_o(1, T.TBP, [(T.MSG, 0, [(s_msg, 1)])])
+        g.wait_ge(s_op, 1)
+        loc += send(g, T, topo, core, [(R["h1"], cd(T.OC, 1), cd(T.HC, 0), T.sem.hc0, on)])
+        loc += send(g, T, topo, core, [(R["h1"], sc(T.OS, 1), sc(T.HS, 0), T.sem.hs0, on)])
+    s_own = make_o(0, T.TBL, [(T.MSG, 0, [(s_msg, 1)])])
+    s_tq, s_wq = ev(), ev()
+    V.wait_ge(s_tab, 16)
+    V.quantize_mx(T.TC[:], T.TS[:], T.TAB[:]).then_inc(s_tq, 1)
+    V.wait_ge(s_w, 16)
+    V.quantize_mx(T.WC[:], T.WS[:], T.WB[:]).then_inc(s_wq, 1)
+    P.wait_ge(s_tq, 1)
+    z = mm_z(1, sc(T.OC, 0), sc(T.OS, 0), [(s_own, 1)])
+    s_e0 = make_e(0, 1, *z)
+
+    if big:
+        so = make_o(1, T.TBL, [land(j) for j in near])
+        z = mm_z(3, sc(T.OC, 1, 3), sc(T.OS, 1, 3), [(so, 1)])
+        sq = make_e(1, 3, *z)
+        h = split(off, 2)
+        loc += ship(sq, [via(R["h1"], 1, 0, up), straight(near[1], 2, h[0]), straight(near[2], 3, h[1])])
+        pr = R["pairs"][0]
+        so = make_o(4, T.TBL, [land(j) for j in pr])
+        z = mm_z(2, sc(T.OC, 4, 2), sc(T.OS, 4, 2), [(so, 1)])
+        sq = make_e(4, 2, *z)
+        loc += ship(sq, [via(R["h0"], 4, 1, up), via(R["h1"], 5, 1, off)])
+        order = near[1:] + near[:1] + far
+    else:
+        zs = []
+        for i, pr in enumerate(R["pairs"]):
+            so = make_o(2 + 2 * i, T.TBL, [land(j) for j in pr])
+            zs.append(mm_z(2, sc(T.OC, 2 + 2 * i, 2), sc(T.OS, 2 + 2 * i, 2), [(so, 1)]))
+        for i, zz in enumerate(zs):
+            sq = make_e(2 + 2 * i, 2, *zz)
+            loc += ship(sq, [via(R["h0"], 2 + 2 * i, i + 1, up), via(R["h1"], 3 + 2 * i, i + 1, off)])
+        z = mm_z(1, T.ROC[:], T.ROS[:], [(T.sem.oa, 2 * len(roads[near[0]]["off"]))])
+        sq = make_e(1, 1, *z)
+        loc += ship(sq, [straight(near[0], 1, off)])
+        order = far + near
+
+    s_y, s_ys, s_st = ev(), ev(), ev()
+    P.wait_ge(s_wq, 1)
+    P.wait_ge(s_e0, 1)
+    P.matmul_mx(T.YP[:, 0:NC], T.WC[:], T.WS[:], sc(T.EC, 0), sc(T.ES, 0), True, False)
+    for i, j in enumerate(order):
+        P.wait_ge(T.sem["ee%d" % j], e_count(j))
+        last = i == len(order) - 1
+        c = P.matmul_mx(T.YP[:, 0:NC], T.WC[:], T.WS[:], sc(T.LC, j), sc(T.LS, j), False, last)
+        if last:
+            c.then_inc(s_y, 1)
+    V.wait_ge(s_y, 1)
+    V.tensor_copy(T.YS[:], T.YP[:, 0:NC]).then_inc(s_ys, 1)
+    g.sync.wait_ge(s_ys, 1)
+    g.sync.dma_start(T.y[:], T.YS[:]).then_inc(s_st, 16)
+    g.sync.wait_ge(s_st, 16)
+    g.wait_ge(T.sem.loc, loc)
+
+
+def rank_program(g, core, T, topo):
+    r = T.rank_of(core)
+    if r is not None:
+        rank_core(g, core, r, road(r, T, topo), T, topo)
+        return
+    for r in range(NR):
+        R = road(r, T, topo)
+        if core in (R["h0"], R["h1"]):
+            helper_program(g, core, r, R, T, topo)

@@ -6,7 +6,7 @@ Op = AluOpType
 Act = ActivationFunctionType
 NR = 6
 NC = 128
-NBANK = 7
+NBANK = 8
 LN2 = math.log(2.0)
 
 SCRATCH = {
@@ -18,11 +18,11 @@ SCRATCH = {
     "TS": ("sbuf", [128, 512], "uint8"),
     "WC": ("sbuf", [128, 128], "float8_e4m3fn_x4"),
     "WS": ("sbuf", [128, 128], "uint8"),
-    "IOT": ("sbuf", [128, 32], "bfloat16"),
+    "IOT": ("sbuf", [128, 1], "bfloat16"),
     "KC": ("sbuf", [128, 1], "float32"),
     "KR": ("sbuf", [128, 1], "float32"),
-    "TBL": ("sbuf", [128, 4, 32], "bfloat16"),
-    "TBP": ("sbuf", [128, 4, 32], "bfloat16"),
+    "VT": ("sbuf", [128, 4], "bfloat16"),
+    "VP": ("sbuf", [128, 4], "bfloat16"),
     "E1": ("sbuf", [128, 4], "bfloat16"),
     "E2": ("sbuf", [128, 4], "bfloat16"),
     "P1": ("sbuf", [128, 4], "bfloat16"),
@@ -30,26 +30,26 @@ SCRATCH = {
     "MSG": ("sbuf", [128, 4], "bfloat16"),
     "LAND": ("sbuf", [128, 4 * NR], "bfloat16"),
     "LANDH": ("sbuf", [128, 4], "bfloat16"),
-    "Y3": ("sbuf", [128, 4, NR * NC], "bfloat16"),
-    "O": ("sbuf", [128, NR * 512], "bfloat16"),
-    "OC": ("sbuf", [128, NR * NC], "float8_e4m3fn_x4"),
-    "OS": ("sbuf", [128, NR * NC], "uint8"),
-    "ROC": ("sbuf", [128, NC], "float8_e4m3fn_x4"),
-    "ROS": ("sbuf", [128, NC], "uint8"),
+    "M0": ("sbuf", [128, 3 * NC], "bfloat16"),
+    "D1": ("sbuf", [128, NR * NC], "bfloat16"),
+    "XB": ("sbuf", [128, NR * NC], "bfloat16"),
+    "BI": ("sbuf", [128, NR * NC], "bfloat16"),
+    "O": ("sbuf", [128, 7 * 512], "bfloat16"),
+    "OC": ("sbuf", [128, 7 * NC], "float8_e4m3fn_x4"),
+    "OS": ("sbuf", [128, 7 * NC], "uint8"),
     "ET": ("sbuf", [128, NR * 512], "bfloat16"),
     "EC": ("sbuf", [128, NR * NC], "float8_e4m3fn_x4"),
     "ES": ("sbuf", [128, NR * NC], "uint8"),
     "LC": ("sbuf", [128, NR * NC], "float8_e4m3fn_x4"),
     "LS": ("sbuf", [128, NR * NC], "uint8"),
-    "HC": ("sbuf", [128, 3 * NC], "float8_e4m3fn_x4"),
-    "HS": ("sbuf", [128, 3 * NC], "uint8"),
+    "HC": ("sbuf", [128, 4 * NC], "float8_e4m3fn_x4"),
+    "HS": ("sbuf", [128, 4 * NC], "uint8"),
     "YS": ("sbuf", [128, NC], "float32"),
     "ZP": ("psum", [128, 512 * NBANK], "float32"),
-    "YP": ("psum", [128, 512], "float32"),
 }
-NEV = 90
+NEV = 100
 SEMAPHORES = (["v%d" % i for i in range(NEV)] + ["id%d" % i for i in range(NR)] + ["ee%d" % i for i in range(NR)]
-              + ["hc%d" % i for i in range(3)] + ["hs%d" % i for i in range(3)] + ["idh", "oa", "loc"])
+              + ["hc%d" % i for i in range(4)] + ["hs%d" % i for i in range(4)] + ["idh", "oa", "loc"])
 
 
 def lanes(mask):
@@ -89,8 +89,28 @@ def road(r, T, topo):
     on = lanes(topo.mask(me, h0))
     off = lanes(topo.mask(me, cores[near[0]]))
     up = [e for e in on if e not in off]
-    return {"me": me, "group": group, "far": far, "near": near, "h0": h0, "h1": h1, "pairs": list(zip(a, b)),
-            "on": on, "off": off, "up": up, "big": len(near) > 1}
+    return {"me": me, "far": far, "near": near, "h0": h0, "h1": h1, "pairs": list(zip(a, b)), "off": off, "up": up,
+            "big": len(near) > 1, "get": None, "give": None}
+
+
+def plan(T, topo):
+    roads = [road(j, T, topo) for j in range(NR)]
+    for j, R in enumerate(roads):
+        if not R["big"]:
+            R["get"] = R["pairs"][1][0]
+            roads[R["get"]]["give"] = j
+    pair = [j for j, R in enumerate(roads) if R["big"] and R["give"] is None]
+    for j, k in (pair, pair[::-1]):
+        roads[j]["get"] = roads[j]["give"] = k
+    for j, R in enumerate(roads):
+        near = [x for x in R["near"] if x != R["give"]]
+        R["tell"] = near
+        R["near"] = near + [x for x in R["near"] if x not in near]
+        rel = [x for x in R["far"] if x != R["give"]]
+        R["relay"] = [rel[:2], rel[2:]]
+        R["order"] = [j] + R["near"] + [x for pr in R["pairs"] for x in pr]
+        R["tile"] = {x: t for t, x in enumerate(R["order"])}
+    return roads
 
 
 def send(g, T, topo, src, items):
@@ -112,23 +132,38 @@ def sc(t, i, n=1):
     return t[:, NC * i:NC * (i + n)]
 
 
-def helper_program(g, core, r, R, T, topo):
+def four(t, i):
+    return t[:, 4 * i:4 * i + 4]
+
+
+def to_helpers(R):
+    hs = [h for h, rel in zip(("h0", "h1"), R["relay"]) if rel]
+    return dict(zip(hs, split(R["up"], len(hs))))
+
+
+def helper_program(g, core, r, roads, T, topo):
     cores = T.cores
+    R = roads[r]
     first = core == R["h0"]
+    up, off = len(R["up"]), len(R["off"])
     loc = 0
-    if first:
-        g.wait_ge(T.sem.idh, len(R["up"]))
-        parts = split(R["off"], len(R["far"]))
-        loc += send(g, T, topo, core, [(cores[j], T.LANDH[:], T.LAND[:, 4 * r:4 * r + 4], T.sem["id%d" % r], parts[i])
-                                       for i, j in enumerate(R["far"])])
+    rel = R["relay"][0 if first else 1]
+    if rel:
+        g.wait_ge(T.sem.idh, len(to_helpers(R)["h0" if first else "h1"]))
+        parts = split(R["off"], len(rel))
+        loc += send(g, T, topo, core, [(cores[j], T.LANDH[:], four(T.LAND, roads[j]["tile"][r]), T.sem["id%d" % r], parts[i])
+                                       for i, j in enumerate(rel)])
     todo = []
+    there = (T.LC, T.LS, r)
     if not first:
-        if R["big"]:
-            todo.append((0, len(R["up"]), R["near"][0], (T.LC, T.LS, r), T.sem["ee%d" % r]))
-        else:
-            todo.append((0, len(R["on"]), R["near"][0], (T.ROC, T.ROS, 0), T.sem.oa))
+        j = R["give"]
+        if j is not None:
+            todo.append((3, up, j, (T.OC, T.OS, roads[j]["tile"][r]), T.sem.oa))
+        todo.append((0, up, R["near"][0], there, T.sem["ee%d" % r]))
+    elif R["big"]:
+        todo.append((0, off, R["near"][1], there, T.sem["ee%d" % r]))
     for s, pr in enumerate(R["pairs"]):
-        todo.append((s + 1, len(R["up"] if first else R["off"]), pr[0 if first else 1], (T.LC, T.LS, r), T.sem["ee%d" % r]))
+        todo.append((s + 1, up if first else off, pr[0 if first else 1], there, T.sem["ee%d" % r]))
     for slot, n, j, (bc, bs, at), sem in todo:
         g.wait_ge(T.sem["hc%d" % slot], n)
         loc += send(g, T, topo, core, [(cores[j], cd(T.HC, slot), cd(bc, at), sem, R["off"])])
@@ -137,8 +172,9 @@ def helper_program(g, core, r, R, T, topo):
     g.wait_ge(T.sem.loc, loc)
 
 
-def rank_core(g, core, r, R, T, topo):
+def rank_core(g, core, r, roads, T, topo):
     cores = T.cores
+    R = roads[r]
     V, S, P = g.vector, g.scalar, g.tensor
     cnt = [0]
 
@@ -146,89 +182,106 @@ def rank_core(g, core, r, R, T, topo):
         cnt[0] += 1
         return T.sem["v%d" % (cnt[0] - 1)]
 
-    near, far, big = R["near"], R["far"], R["big"]
-    on, off, up = R["on"], R["off"], R["up"]
-    roads = [road(j, T, topo) for j in range(NR)]
+    near, big, give, get = R["near"], R["big"], R["give"], R["get"]
+    off, up = R["off"], R["up"]
 
     def id_count(j):
-        if j in near:
-            k = roads[j]["near"].index(r)
-            return len(split(roads[j]["off"], len(roads[j]["near"]))[k])
-        k = roads[j]["far"].index(r)
-        return len(split(roads[j]["off"], len(roads[j]["far"]))[k])
-
-    def e_count(j):
         Q = roads[j]
-        if j in near and Q["big"] and Q["near"].index(r) > 0:
-            return 2 * len(split(Q["off"], 2)[0])
-        return 2 * len(Q["off"])
+        for way in [Q["tell"]] + Q["relay"]:
+            if r in way:
+                return len(split(Q["off"], len(way))[way.index(r)])
 
     s_tg, s_tab, s_w = ev(), ev(), ev()
     g.sync.dma_start(T.TG[:], T.tg[:]).then_inc(s_tg, 16)
     g.sync.dma_start(T.TAB[:], T.tab[:]).then_inc(s_tab, 16)
     g.sync.dma_start(T.WB[:], T.w[:]).then_inc(s_w, 16)
 
-    s_io = ev()
-    for a in range(4):
-        g.iota(T.IOT[32 * a:32 * a + 32, :], [[1, 32]], 32 * a + 1, 0, allow_small_or_imprecise_dtypes=True).then_inc(s_io, 1)
-
-    s_kc, s_kr = ev(), ev()
+    s_io, s_kc, s_kr, s_m, s_m2 = ev(), ev(), ev(), ev(), ev()
+    g.iota(T.IOT[:], [[1, 1]], 1, 1, allow_small_or_imprecise_dtypes=True).then_inc(s_io, 1)
     V.memset(T.KC[:], float(r)).then_inc(s_kc, 1)
     S.wait_ge(s_kc, 1)
     S.activation(T.KR[:], T.KC[:], Act.Exp, bias=-95.0 * LN2, scale=32.0 * LN2).then_inc(s_kr, 1)
+    V.memset(T.M0[:], 1.0).then_inc(s_m, 1)
+    V.memset(T.D1[:], 0.0).then_inc(s_m, 1)
+    V.wait_ge(s_m, 2)
+    V.memset(T.M0[:, 0:3 * NC:32], 0.0).then_inc(s_m2, 1)
 
-    s_t, s_e, s_p, s_x, s_msg = ev(), ev(), ev(), ev(), ev()
+    s_tb, s_t, s_tp, s_e2, s_e1, s_p, s_x, s_msg = ev(), ev(), ev(), ev(), ev(), ev(), ev(), ev()
     V.wait_ge(s_tg, 16)
-    V.transpose(T.TGT[:], T.TG[:]).then_inc(s_t, 1)
+    V.transpose(T.TGT[:, 256:384], T.TG[:, 256:384]).then_inc(s_tb, 1)
+    V.transpose(T.TGT[:, 0:128], T.TG[:, 0:128]).then_inc(s_t, 1)
+    V.transpose(T.TGT[:, 128:256], T.TG[:, 128:256]).then_inc(s_tp, 1)
+    S.wait_ge(s_tb, 1)
+    S.activation(T.E2[:], T.TGT[:, 256:384:32], Act.Exp, scale=8.0 * LN2).then_inc(s_e2, 1)
     S.wait_ge(s_t, 1)
-    S.activation(T.E2[:], T.TGT[:, 256:384:32], Act.Exp, scale=8.0 * LN2).then_inc(s_e, 1)
-    S.activation(T.E1[:], T.TGT[:, 0:128:32], Act.Exp, bias=-95.0 * LN2, scale=32.0 * LN2).then_inc(s_e, 1)
-    V.wait_ge(s_t, 1)
+    S.activation(T.E1[:], T.TGT[:, 0:128:32], Act.Exp, bias=-95.0 * LN2, scale=32.0 * LN2).then_inc(s_e1, 1)
+    V.wait_ge(s_tp, 1)
     V.tensor_scalar(T.P1[:], T.TGT[:, 128:256:32], 1.0, None, Op.add).then_inc(s_p, 1)
     V.wait_ge(s_p, 1)
-    V.wait_ge(s_e, 2)
+    V.wait_ge(s_e2, 1)
     V.tensor_tensor(T.X[:], T.P1[:], T.E2[:], Op.mult).then_inc(s_x, 1)
     V.wait_ge(s_x, 1)
+    V.wait_ge(s_e1, 1)
     V.tensor_tensor(T.MSG[:], T.X[:], T.E1[:], Op.mult).then_inc(s_msg, 1)
 
     loc = 0
     g.wait_ge(s_msg, 1)
-    loc += send(g, T, topo, core, [(R["h0"], T.MSG[:], T.LANDH[:], T.sem.idh, up)])
-    if big:
-        parts = split(off, len(near))
-        loc += send(g, T, topo, core, [(cores[j], T.MSG[:], T.LAND[:, 4 * r:4 * r + 4], T.sem["id%d" % r], parts[i])
-                                       for i, j in enumerate(near)])
+    loc += send(g, T, topo, core, [(R[h], T.MSG[:], T.LANDH[:], T.sem.idh, es) for h, es in to_helpers(R).items()])
+    parts = split(off, len(R["tell"]))
+    loc += send(g, T, topo, core, [(cores[j], T.MSG[:], four(T.LAND, roads[j]["tile"][r]), T.sem["id%d" % r], parts[i])
+                                   for i, j in enumerate(R["tell"])])
 
-    V.wait_ge(s_io, 4)
+    V.wait_ge(s_msg, 1)
+    V.wait_ge(s_io, 1)
     V.wait_ge(s_kr, 1)
-    s_tb = ev()
+    V.wait_ge(s_m2, 1)
+    s_vt, s_vp = ev(), ev()
     for b in range(4):
-        V.tensor_scalar(T.TBL[:, b, :], T.IOT[:], float(2.0 ** (8 * b)), T.KR[:], Op.mult, Op.mult).then_inc(s_tb, 1)
-    if not big:
-        s_tp = ev()
+        V.tensor_scalar(T.VT[:, b:b + 1], T.IOT[:], float(2.0 ** (8 * b)), T.KR[:], Op.mult, Op.mult).then_inc(s_vt, 1)
+    if give is not None:
         for b in range(4):
-            V.tensor_scalar(T.TBP[:, b, :], T.IOT[:], float(2.0 ** (8 * b + 32 * (near[0] - r))), T.KR[:], Op.mult, Op.mult).then_inc(s_tp, 1)
+            V.tensor_scalar(T.VP[:, b:b + 1], T.IOT[:], float(2.0 ** (8 * b + 32 * (give - r))), T.KR[:],
+                            Op.mult, Op.mult).then_inc(s_vp, 1)
+        V.wait_ge(s_vp, 4)
+    V.wait_ge(s_vt, 4)
 
-    def make_o(t0, tab, srcs):
-        n = len(srcs)
-        s_y, s_o, s_q = ev(), ev(), ev()
-        for i, (buf, c0, waits) in enumerate(srcs):
-            for sem, val in waits:
-                V.wait_ge(sem, val)
-            for k in range(4):
-                at = NC * (t0 + i) + 32 * k
-                V.tensor_scalar(T.Y3[:, :, at:at + 32], tab[:], buf[:, c0 + k:c0 + k + 1], None, Op.is_equal).then_inc(s_y, 1)
-        V.wait_ge(s_y, 4 * n)
+    def spread(t, n, buf, c0):
+        s_d, s_s, s_b = ev(), ev(), ev()
+        V.tensor_copy(T.D1[:, NC * t:NC * (t + n):32], buf[:, c0:c0 + 4 * n]).then_inc(s_d, 1)
+        V.wait_ge(s_d, 1)
+        V.tensor_tensor_scan(sc(T.XB, t, n), sc(T.M0, 0, n), sc(T.D1, t, n), 0.0, Op.mult, Op.add).then_inc(s_s, 1)
+        V.wait_ge(s_s, 1)
+        V.transpose(sc(T.BI, t, n), sc(T.XB, t, n)).then_inc(s_b, 1)
+        V.wait_ge(s_b, 1)
+
+    def ones(to, t, n, tab):
+        s_o, s_q = ev(), ev()
         for b in range(4):
-            V.transpose(T.O[:, 512 * t0 + b:512 * (t0 + n):4], T.Y3[:, b, NC * t0:NC * (t0 + n)]).then_inc(s_o, 1)
+            V.tensor_scalar(T.O[:, 512 * to + b:512 * (to + n):4], sc(T.BI, t, n), tab[:, b:b + 1], None, Op.is_equal).then_inc(s_o, 1)
         V.wait_ge(s_o, 4)
-        V.quantize_mx(sc(T.OC, t0, n), sc(T.OS, t0, n), T.O[:, 512 * t0:512 * (t0 + n)]).then_inc(s_q, 1)
+        V.quantize_mx(sc(T.OC, to, n), sc(T.OS, to, n), T.O[:, 512 * to:512 * (to + n)]).then_inc(s_q, 1)
         return s_q
+
+    def make_o(t, n):
+        js = R["order"][t:t + n]
+        waits = []
+        if get in js:
+            waits.append((T.sem.oa, 2 * len(off)))
+            if n > 1:
+                t, n, js = (t + 1, n - 1, js[1:]) if js[0] == get else (t, n - 1, js[:-1])
+            else:
+                n = 0
+        if n:
+            for j in js:
+                V.wait_ge(T.sem["id%d" % j], id_count(j))
+            spread(t, n, T.LAND, 4 * t)
+            waits.append((ones(t, t, n, T.VT), 1))
+        return waits
 
     bank = [0]
     busy = {}
 
-    def mm_z(n, oc, os_, waits):
+    def mm_z(t, n, waits):
         s_c = ev()
         mine = "v%d" % (cnt[0] - 1)
         res = []
@@ -243,27 +296,25 @@ def rank_core(g, core, r, R, T, topo):
                 seen.append(busy[k])
             busy[k] = mine
             s_z = ev()
-            P.matmul_mx(T.ZP[:, 512 * k:512 * k + NC * n], sc(T.TC, f), sc(T.TS, f), oc, os_, True, True).then_inc(s_z, 1)
+            P.matmul_mx(T.ZP[:, 512 * k:512 * k + NC * n], sc(T.TC, f), sc(T.TS, f), sc(T.OC, t, n), sc(T.OS, t, n), True, True).then_inc(s_z, 1)
             res.append((k, s_z))
         return res, s_c
 
-    def make_e(t0, n, res, s_c):
+    def make_e(t, n, z, on_v):
+        res, s_c = z
         s_q = ev()
         for f, (k, s_z) in enumerate(res):
             src = T.ZP[:, 512 * k:512 * k + NC * n]
-            out = T.ET[:, 512 * t0 + f:512 * (t0 + n):4]
-            if f % 2:
-                S.wait_ge(s_z, 1)
-                S.activation(out, src, Act.Copy).then_inc(s_c, 1)
-            else:
+            out = T.ET[:, 512 * t + f:512 * (t + n):4]
+            if f in on_v:
                 V.wait_ge(s_z, 1)
                 V.tensor_copy(out, src).then_inc(s_c, 1)
+            else:
+                S.wait_ge(s_z, 1)
+                S.activation(out, src, Act.Copy).then_inc(s_c, 1)
         V.wait_ge(s_c, 4)
-        V.quantize_mx(sc(T.EC, t0, n), sc(T.ES, t0, n), T.ET[:, 512 * t0:512 * (t0 + n)]).then_inc(s_q, 1)
+        V.quantize_mx(sc(T.EC, t, n), sc(T.ES, t, n), T.ET[:, 512 * t:512 * (t + n)]).then_inc(s_q, 1)
         return s_q
-
-    def land(j):
-        return (T.LAND, 4 * j, [(T.sem["id%d" % j], id_count(j))])
 
     def ship(s_q, items):
         g.wait_ge(s_q, 1)
@@ -271,66 +322,67 @@ def rank_core(g, core, r, R, T, topo):
         return a + send(g, T, topo, core, [(d, sc(T.ES, t), sc(bs, at), s2, es) for d, t, bc, bs, at, s1, s2, es in items])
 
     def via(h, t, slot, es):
-        return (h, t, T.HC, T.HS, slot, T.sem["hc%d" % slot], T.sem["hs%d" % slot], es)
+        return (R[h], t, T.HC, T.HS, slot, T.sem["hc%d" % slot], T.sem["hs%d" % slot], es)
 
-    def straight(j, t, es):
-        sem = T.sem["ee%d" % r]
-        return (cores[j], t, T.LC, T.LS, r, sem, sem, es)
-
-    V.wait_ge(s_tb, 4)
-    if not big:
-        V.wait_ge(s_tp, 4)
-        s_op = make_o(1, T.TBP, [(T.MSG, 0, [(s_msg, 1)])])
-        g.wait_ge(s_op, 1)
-        loc += send(g, T, topo, core, [(R["h1"], cd(T.OC, 1), cd(T.HC, 0), T.sem.hc0, on)])
-        loc += send(g, T, topo, core, [(R["h1"], sc(T.OS, 1), sc(T.HS, 0), T.sem.hs0, on)])
-    s_own = make_o(0, T.TBL, [(T.MSG, 0, [(s_msg, 1)])])
+    if give is not None:
+        spread(0, 1, T.MSG, 0)
+        s_g = ones(6, 0, 1, T.VP)
+        g.wait_ge(s_g, 1)
+        loc += send(g, T, topo, core, [(R["h1"], cd(T.OC, 6), cd(T.HC, 3), T.sem.hc3, up)])
+        loc += send(g, T, topo, core, [(R["h1"], sc(T.OS, 6), sc(T.HS, 3), T.sem.hs3, up)])
     s_tq, s_wq = ev(), ev()
     V.wait_ge(s_tab, 16)
     V.quantize_mx(T.TC[:], T.TS[:], T.TAB[:]).then_inc(s_tq, 1)
+    P.wait_ge(s_tq, 1)
+
+    m = len(near)
+    t = 1 + m
+    if big:
+        z = mm_z(1, 2, make_o(1, 2))
+        zx = mm_z(t, 2, make_o(t, 2))
+        sq = make_e(1, 2, z, ())
+        loc += ship(sq, [via("h1", 1, 0, up), via("h0", 2, 0, off)])
+        z = mm_z(3, 1, make_o(3, 1))
+        sq = make_e(t, 2, zx, (1, 3))
+        loc += ship(sq, [via("h0", t, 1, up), via("h1", t + 1, 1, off)])
+        sq = make_e(3, 1, z, ())
+        sem = T.sem["ee%d" % r]
+        loc += ship(sq, [(cores[near[2]], 3, T.LC, T.LS, r, sem, sem, off)])
+    else:
+        z = mm_z(1, m, make_o(1, m))
+        sq = make_e(1, m, z, (0, 2))
+        loc += ship(sq, [via("h1", 1, 0, up)])
+        z = mm_z(t, 2, make_o(t, 2))
+        z2 = mm_z(t + 2, 2, make_o(t + 2, 2))
+        sq = make_e(t, 2, z, (3,))
+        loc += ship(sq, [via("h0", t, 1, up), via("h1", t + 1, 1, off)])
+        sq = make_e(t + 2, 2, z2, (1, 3))
+        loc += ship(sq, [via("h0", t + 2, 2, up), via("h1", t + 3, 2, off)])
+
+    if give is None:
+        spread(0, 1, T.MSG, 0)
+    s_own = ones(0, 0, 1, T.VT)
     V.wait_ge(s_w, 16)
     V.quantize_mx(T.WC[:], T.WS[:], T.WB[:]).then_inc(s_wq, 1)
-    P.wait_ge(s_tq, 1)
-    z = mm_z(1, sc(T.OC, 0), sc(T.OS, 0), [(s_own, 1)])
-    s_e0 = make_e(0, 1, *z)
-
-    if big:
-        so = make_o(1, T.TBL, [land(j) for j in near])
-        z = mm_z(3, sc(T.OC, 1, 3), sc(T.OS, 1, 3), [(so, 1)])
-        sq = make_e(1, 3, *z)
-        h = split(off, 2)
-        loc += ship(sq, [via(R["h1"], 1, 0, up), straight(near[1], 2, h[0]), straight(near[2], 3, h[1])])
-        pr = R["pairs"][0]
-        so = make_o(4, T.TBL, [land(j) for j in pr])
-        z = mm_z(2, sc(T.OC, 4, 2), sc(T.OS, 4, 2), [(so, 1)])
-        sq = make_e(4, 2, *z)
-        loc += ship(sq, [via(R["h0"], 4, 1, up), via(R["h1"], 5, 1, off)])
-        order = near[1:] + near[:1] + far
-    else:
-        zs = []
-        for i, pr in enumerate(R["pairs"]):
-            so = make_o(2 + 2 * i, T.TBL, [land(j) for j in pr])
-            zs.append(mm_z(2, sc(T.OC, 2 + 2 * i, 2), sc(T.OS, 2 + 2 * i, 2), [(so, 1)]))
-        for i, zz in enumerate(zs):
-            sq = make_e(2 + 2 * i, 2, *zz)
-            loc += ship(sq, [via(R["h0"], 2 + 2 * i, i + 1, up), via(R["h1"], 3 + 2 * i, i + 1, off)])
-        z = mm_z(1, T.ROC[:], T.ROS[:], [(T.sem.oa, 2 * len(roads[near[0]]["off"]))])
-        sq = make_e(1, 1, *z)
-        loc += ship(sq, [straight(near[0], 1, off)])
-        order = far + near
+    z = mm_z(0, 1, [(s_own, 1)])
+    s_e0 = make_e(0, 1, z, (0, 2))
 
     s_y, s_ys, s_st = ev(), ev(), ev()
+    k = bank[0] % NBANK
+    yp = T.ZP[:, 512 * k:512 * k + NC]
     P.wait_ge(s_wq, 1)
+    P.wait_ge(T.sem[busy[k]], 4)
     P.wait_ge(s_e0, 1)
-    P.matmul_mx(T.YP[:, 0:NC], T.WC[:], T.WS[:], sc(T.EC, 0), sc(T.ES, 0), True, False)
+    P.matmul_mx(yp, T.WC[:], T.WS[:], sc(T.EC, 0), sc(T.ES, 0), True, False)
+    order = R["order"][1:]
     for i, j in enumerate(order):
-        P.wait_ge(T.sem["ee%d" % j], e_count(j))
+        P.wait_ge(T.sem["ee%d" % j], 2 * len(off))
         last = i == len(order) - 1
-        c = P.matmul_mx(T.YP[:, 0:NC], T.WC[:], T.WS[:], sc(T.LC, j), sc(T.LS, j), False, last)
+        c = P.matmul_mx(yp, T.WC[:], T.WS[:], sc(T.LC, j), sc(T.LS, j), False, last)
         if last:
             c.then_inc(s_y, 1)
     V.wait_ge(s_y, 1)
-    V.tensor_copy(T.YS[:], T.YP[:, 0:NC]).then_inc(s_ys, 1)
+    V.tensor_copy(T.YS[:], yp).then_inc(s_ys, 1)
     g.sync.wait_ge(s_ys, 1)
     g.sync.dma_start(T.y[:], T.YS[:]).then_inc(s_st, 16)
     g.sync.wait_ge(s_st, 16)
@@ -338,11 +390,11 @@ def rank_core(g, core, r, R, T, topo):
 
 
 def rank_program(g, core, T, topo):
+    roads = plan(T, topo)
     r = T.rank_of(core)
     if r is not None:
-        rank_core(g, core, r, road(r, T, topo), T, topo)
+        rank_core(g, core, r, roads, T, topo)
         return
     for r in range(NR):
-        R = road(r, T, topo)
-        if core in (R["h0"], R["h1"]):
-            helper_program(g, core, r, R, T, topo)
+        if core in (roads[r]["h0"], roads[r]["h1"]):
+            helper_program(g, core, r, roads, T, topo)

@@ -6,8 +6,18 @@ Op = AluOpType
 Act = ActivationFunctionType
 NR = 6
 NC = 128
-NBANK = 8
 LN2 = math.log(2.0)
+
+STEPS = {
+    "big": ["own", "give", "tab", "come 1 3", "k 1", "o 1", "k 2", "z 1", "k 3", "z 2", "o 2", "come 5 1", "s 1 0 1 2 3",
+            "ship 1 h1 u", "e 1", "v 2 0 1 2", "k 5", "o 3", "o 5", "z 4", "e 2", "z 5", "z 3", "ship 2 h0 a", "w", "e 4", "e 5",
+            "s 2 3", "ship 4 h0 a", "s 4 0 1 2 3", "s 5 0 1 2 3", "ship 5 h1 a", "k 0", "o 0", "z 0", "e 3", "v 0 0 1 2 3", "e 0",
+            "ship 3 - o", "s 3 0 1 2 3"],
+    "small": ["own", "give", "come 1 1", "tab", "k 1", "z 1", "z 2", "o 1", "come 3 3", "z 3", "s 1 0 1 2 3", "k 3", "z 4",
+              "s 2 0 1 2 3", "e 1", "o 3", "ship 1 h0 a", "k 4", "e 2", "o 4", "s 3 0 1 2 3", "k 5", "o 5", "ship 2 h0 a", "e 3",
+              "z 5", "z 0", "v 4 1", "ship 3 h1 a", "s 4 0 2 3", "k 0", "ship 4 h0 a", "e 4", "ship 5 h1 a", "o 0",
+              "s 5 0 1 2 3", "w", "e 5", "s 0 0 1 2 3", "e 0"],
+}
 
 SCRATCH = {
     "TG": ("sbuf", [128, 384], "bfloat16"),
@@ -19,10 +29,11 @@ SCRATCH = {
     "WC": ("sbuf", [128, 128], "float8_e4m3fn_x4"),
     "WS": ("sbuf", [128, 128], "uint8"),
     "IOT": ("sbuf", [128, 1], "bfloat16"),
+    "C4": ("sbuf", [128, 4], "bfloat16"),
     "KC": ("sbuf", [128, 1], "float32"),
     "KR": ("sbuf", [128, 1], "float32"),
     "VT": ("sbuf", [128, 4], "bfloat16"),
-    "VP": ("sbuf", [128, 4], "bfloat16"),
+    "VP": ("sbuf", [128, 8], "bfloat16"),
     "E1": ("sbuf", [128, 4], "bfloat16"),
     "E2": ("sbuf", [128, 4], "bfloat16"),
     "P1": ("sbuf", [128, 4], "bfloat16"),
@@ -34,29 +45,30 @@ SCRATCH = {
     "D1": ("sbuf", [128, NR * NC], "bfloat16"),
     "XB": ("sbuf", [128, NR * NC], "bfloat16"),
     "BI": ("sbuf", [128, NR * NC], "bfloat16"),
-    "O": ("sbuf", [128, 7 * 512], "bfloat16"),
-    "OC": ("sbuf", [128, 7 * NC], "float8_e4m3fn_x4"),
-    "OS": ("sbuf", [128, 7 * NC], "uint8"),
+    "O": ("sbuf", [128, 8 * 512], "bfloat16"),
+    "OC": ("sbuf", [128, 8 * NC], "float8_e4m3fn_x4"),
+    "OS": ("sbuf", [128, 8 * NC], "uint8"),
     "ET": ("sbuf", [128, NR * 512], "bfloat16"),
     "EC": ("sbuf", [128, NR * NC], "float8_e4m3fn_x4"),
     "ES": ("sbuf", [128, NR * NC], "uint8"),
     "LC": ("sbuf", [128, NR * NC], "float8_e4m3fn_x4"),
     "LS": ("sbuf", [128, NR * NC], "uint8"),
-    "HC": ("sbuf", [128, 4 * NC], "float8_e4m3fn_x4"),
-    "HS": ("sbuf", [128, 4 * NC], "uint8"),
+    "HC": ("sbuf", [128, NR * NC], "float8_e4m3fn_x4"),
+    "HS": ("sbuf", [128, NR * NC], "uint8"),
     "YS": ("sbuf", [128, NC], "float32"),
-    "ZP": ("psum", [128, 512 * NBANK], "float32"),
+    "ZP": ("psum", [128, 512 * 8], "float32"),
 }
-NEV = 100
-SEMAPHORES = (["v%d" % i for i in range(NEV)] + ["id%d" % i for i in range(NR)] + ["ee%d" % i for i in range(NR)]
-              + ["hc%d" % i for i in range(4)] + ["hs%d" % i for i in range(4)] + ["idh", "oa", "loc"])
+NEV = 44
+SEMAPHORES = (["v%d" % i for i in range(NEV)]
+              + ["%s%d" % (k, i) for k in ("id", "ee", "hc", "hs", "k", "o", "c", "q") for i in range(NR)]
+              + ["z%d" % i for i in range(4 * NR)] + ["idh", "oa", "loc"])
 
 
 def lanes(mask):
     return [e for e in range(mask.bit_length()) if (mask >> e) & 1]
 
 
-def pack(es):
+def engine_mask(es):
     return sum(1 << e for e in es)
 
 
@@ -89,27 +101,32 @@ def road(r, T, topo):
     on = lanes(topo.mask(me, h0))
     off = lanes(topo.mask(me, cores[near[0]]))
     up = [e for e in on if e not in off]
-    return {"me": me, "far": far, "near": near, "h0": h0, "h1": h1, "pairs": list(zip(a, b)), "off": off, "up": up,
-            "big": len(near) > 1, "get": None, "give": None}
+    return {"me": me, "far": far, "near": near, "h0": h0, "h1": h1, "pairs": list(zip(a, b))[::-1], "off": off, "up": up,
+            "big": len(near) > 1}
 
 
 def plan(T, topo):
     roads = [road(j, T, topo) for j in range(NR)]
-    for j, R in enumerate(roads):
+    for R in roads:
         if not R["big"]:
-            R["get"] = R["pairs"][1][0]
-            roads[R["get"]]["give"] = j
-    pair = [j for j, R in enumerate(roads) if R["big"] and R["give"] is None]
-    for j, k in (pair, pair[::-1]):
-        roads[j]["get"] = roads[j]["give"] = k
+            R["get"] = R["pairs"][0][0]
+            R["give"] = [pr[0] for pr in R["pairs"]]
     for j, R in enumerate(roads):
-        near = [x for x in R["near"] if x != R["give"]]
-        R["tell"] = near
-        R["near"] = near + [x for x in R["near"] if x not in near]
-        rel = [x for x in R["far"] if x != R["give"]]
-        R["relay"] = [rel[:2], rel[2:]]
+        if R["big"]:
+            R["get"] = [k for k in R["far"] if j in roads[k]["give"]][0]
+            R["give"] = [k for k in R["far"] if roads[k]["get"] == j]
+            R["pairs"] = [(R["get"], [k for k in R["far"] if k != R["get"]][0])]
+    for j, R in enumerate(roads):
+        rel = [x for x in R["far"] if x not in R["give"]]
+        R["relay"] = {"h0": rel[:1], "h1": rel[1:]}
+        R["made"] = {"h0": R["give"][:1], "h1": R["give"][1:]}
         R["order"] = [j] + R["near"] + [x for pr in R["pairs"] for x in pr]
         R["tile"] = {x: t for t, x in enumerate(R["order"])}
+        R["steps"] = [w.split() for w in STEPS["big" if R["big"] else "small"]]
+        R["ways"] = []
+        for w in R["steps"]:
+            if w[0] == "ship":
+                R["ways"].append((int(w[1]), w[2], {"u": R["up"], "o": R["off"], "a": R["off"] + R["up"]}[w[3]]))
     return roads
 
 
@@ -118,14 +135,14 @@ def send(g, T, topo, src, items):
     n = 0
     for d, s, o, sem, es in items:
         rid, pid = topo.addr(d, src)
-        tr.append(RemoteDMATransfer(dst_ids=[DstId(rid=rid, pnc=pid)], dma_engine_mask=pack(es), remote_sem=sem, src=s, dst=o))
+        tr.append(RemoteDMATransfer(dst_ids=[DstId(rid=rid, pnc=pid)], dma_engine_mask=engine_mask(es), remote_sem=sem, src=s, dst=o))
         n += len(es)
     g.remote_dma_fused(tr, local_sem=T.sem.loc)
     return n
 
 
-def cd(t, i, n=1):
-    return t[:, NC * i:NC * (i + n)].bitcast(dt.uint8)
+def cd(t, i):
+    return t[:, NC * i:NC * (i + 1)].bitcast(dt.uint8)
 
 
 def sc(t, i, n=1):
@@ -137,38 +154,25 @@ def four(t, i):
 
 
 def to_helpers(R):
-    hs = [h for h, rel in zip(("h0", "h1"), R["relay"]) if rel]
+    hs = [h for h in ("h0", "h1") if R["relay"][h]]
     return dict(zip(hs, split(R["up"], len(hs))))
 
 
 def helper_program(g, core, r, roads, T, topo):
     cores = T.cores
     R = roads[r]
-    first = core == R["h0"]
-    up, off = len(R["up"]), len(R["off"])
+    me = "h0" if core == R["h0"] else "h1"
     loc = 0
-    rel = R["relay"][0 if first else 1]
-    if rel:
-        g.wait_ge(T.sem.idh, len(to_helpers(R)["h0" if first else "h1"]))
-        parts = split(R["off"], len(rel))
-        loc += send(g, T, topo, core, [(cores[j], T.LANDH[:], four(T.LAND, roads[j]["tile"][r]), T.sem["id%d" % r], parts[i])
-                                       for i, j in enumerate(rel)])
-    todo = []
-    there = (T.LC, T.LS, r)
-    if not first:
-        j = R["give"]
-        if j is not None:
-            todo.append((3, up, j, (T.OC, T.OS, roads[j]["tile"][r]), T.sem.oa))
-        todo.append((0, up, R["near"][0], there, T.sem["ee%d" % r]))
-    elif R["big"]:
-        todo.append((0, off, R["near"][1], there, T.sem["ee%d" % r]))
-    for s, pr in enumerate(R["pairs"]):
-        todo.append((s + 1, up if first else off, pr[0 if first else 1], there, T.sem["ee%d" % r]))
-    for slot, n, j, (bc, bs, at), sem in todo:
-        g.wait_ge(T.sem["hc%d" % slot], n)
-        loc += send(g, T, topo, core, [(cores[j], cd(T.HC, slot), cd(bc, at), sem, R["off"])])
-        g.wait_ge(T.sem["hs%d" % slot], n)
-        loc += send(g, T, topo, core, [(cores[j], sc(T.HS, slot), sc(bs, at), sem, R["off"])])
+    for j in R["relay"][me]:
+        g.wait_ge(T.sem.idh, len(to_helpers(R)[me]))
+        loc += send(g, T, topo, core, [(cores[j], T.LANDH[:], four(T.LAND, roads[j]["tile"][r]), T.sem["id%d" % r], R["off"])])
+    todo = [(0, R["up" if me == "h0" else "off"], j, (T.OC, T.OS, roads[j]["tile"][r]), T.sem.oa) for j in R["made"][me]]
+    todo += [(t, es, R["order"][t], (T.LC, T.LS, r), T.sem["ee%d" % r]) for t, h, es in R["ways"] if h == me]
+    for t, es, j, (bc, bs, at), sem in todo:
+        g.wait_ge(T.sem["hs%d" % t], len(es))
+        loc += send(g, T, topo, core, [(cores[j], sc(T.HS, t), sc(bs, at), sem, R["off"])])
+        g.wait_ge(T.sem["hc%d" % t], len(es))
+        loc += send(g, T, topo, core, [(cores[j], cd(T.HC, t), cd(bc, at), sem, R["off"])])
     g.wait_ge(T.sem.loc, loc)
 
 
@@ -182,35 +186,38 @@ def rank_core(g, core, r, roads, T, topo):
         cnt[0] += 1
         return T.sem["v%d" % (cnt[0] - 1)]
 
-    near, big, give, get = R["near"], R["big"], R["give"], R["get"]
+    near, give, get = R["near"], R["give"], R["get"]
     off, up = R["off"], R["up"]
 
     def id_count(j):
         Q = roads[j]
-        for way in [Q["tell"]] + Q["relay"]:
-            if r in way:
-                return len(split(Q["off"], len(way))[way.index(r)])
+        if r in Q["near"]:
+            return len(split(Q["off"], len(Q["near"]))[Q["near"].index(r)])
+        return len(Q["off"])
 
     s_tg, s_tab, s_w = ev(), ev(), ev()
     g.sync.dma_start(T.TG[:], T.tg[:]).then_inc(s_tg, 16)
     g.sync.dma_start(T.TAB[:], T.tab[:]).then_inc(s_tab, 16)
     g.sync.dma_start(T.WB[:], T.w[:]).then_inc(s_w, 16)
 
-    s_io, s_kc, s_kr, s_m, s_m2 = ev(), ev(), ev(), ev(), ev()
+    s_io, s_kc, s_kr, s_m, s_m2, s_c4 = ev(), ev(), ev(), ev(), ev(), ev()
     g.iota(T.IOT[:], [[1, 1]], 1, 1, allow_small_or_imprecise_dtypes=True).then_inc(s_io, 1)
     V.memset(T.KC[:], float(r)).then_inc(s_kc, 1)
     S.wait_ge(s_kc, 1)
     S.activation(T.KR[:], T.KC[:], Act.Exp, bias=-95.0 * LN2, scale=32.0 * LN2).then_inc(s_kr, 1)
     V.memset(T.M0[:], 1.0).then_inc(s_m, 1)
     V.memset(T.D1[:], 0.0).then_inc(s_m, 1)
+    V.wait_ge(s_io, 1)
+    for b in range(4):
+        V.tensor_scalar(T.C4[:, b:b + 1], T.IOT[:], float(2.0 ** (8 * b)), None, Op.mult).then_inc(s_c4, 1)
     V.wait_ge(s_m, 2)
     V.memset(T.M0[:, 0:3 * NC:32], 0.0).then_inc(s_m2, 1)
 
     s_tb, s_t, s_tp, s_e2, s_e1, s_p, s_x, s_msg = ev(), ev(), ev(), ev(), ev(), ev(), ev(), ev()
     V.wait_ge(s_tg, 16)
     V.transpose(T.TGT[:, 256:384], T.TG[:, 256:384]).then_inc(s_tb, 1)
-    V.transpose(T.TGT[:, 0:128], T.TG[:, 0:128]).then_inc(s_t, 1)
     V.transpose(T.TGT[:, 128:256], T.TG[:, 128:256]).then_inc(s_tp, 1)
+    V.transpose(T.TGT[:, 0:128], T.TG[:, 0:128]).then_inc(s_t, 1)
     S.wait_ge(s_tb, 1)
     S.activation(T.E2[:], T.TGT[:, 256:384:32], Act.Exp, scale=8.0 * LN2).then_inc(s_e2, 1)
     S.wait_ge(s_t, 1)
@@ -227,23 +234,19 @@ def rank_core(g, core, r, roads, T, topo):
     loc = 0
     g.wait_ge(s_msg, 1)
     loc += send(g, T, topo, core, [(R[h], T.MSG[:], T.LANDH[:], T.sem.idh, es) for h, es in to_helpers(R).items()])
-    parts = split(off, len(R["tell"]))
+    parts = split(off, len(near))
     loc += send(g, T, topo, core, [(cores[j], T.MSG[:], four(T.LAND, roads[j]["tile"][r]), T.sem["id%d" % r], parts[i])
-                                   for i, j in enumerate(R["tell"])])
+                                   for i, j in enumerate(near)])
 
-    V.wait_ge(s_msg, 1)
-    V.wait_ge(s_io, 1)
+    s_vt = ev()
+    V.wait_ge(s_c4, 4)
     V.wait_ge(s_kr, 1)
     V.wait_ge(s_m2, 1)
-    s_vt, s_vp = ev(), ev()
-    for b in range(4):
-        V.tensor_scalar(T.VT[:, b:b + 1], T.IOT[:], float(2.0 ** (8 * b)), T.KR[:], Op.mult, Op.mult).then_inc(s_vt, 1)
-    if give is not None:
-        for b in range(4):
-            V.tensor_scalar(T.VP[:, b:b + 1], T.IOT[:], float(2.0 ** (8 * b + 32 * (give - r))), T.KR[:],
-                            Op.mult, Op.mult).then_inc(s_vp, 1)
-        V.wait_ge(s_vp, 4)
-    V.wait_ge(s_vt, 4)
+    for i, k in enumerate(give):
+        V.tensor_scalar(four(T.VP, i), T.C4[:], T.KR[:], float(2.0 ** (32 * (k - r))), Op.mult, Op.mult).then_inc(s_vt, 1)
+    V.tensor_scalar(T.VT[:], T.C4[:], T.KR[:], None, Op.mult).then_inc(s_vt, 1)
+    V.wait_ge(s_msg, 1)
+    V.wait_ge(s_vt, 1 + len(give))
 
     def spread(t, n, buf, c0):
         s_d, s_s, s_b = ev(), ev(), ev()
@@ -254,125 +257,109 @@ def rank_core(g, core, r, roads, T, topo):
         V.transpose(sc(T.BI, t, n), sc(T.XB, t, n)).then_inc(s_b, 1)
         V.wait_ge(s_b, 1)
 
-    def ones(to, t, n, tab):
-        s_o, s_q = ev(), ev()
+    def come(t, n):
+        for j in R["order"][t:t + n]:
+            V.wait_ge(T.sem["id%d" % j], id_count(j))
+        spread(t, n, T.LAND, 4 * t)
+
+    def compare(to, t, num, at, s_o):
         for b in range(4):
-            V.tensor_scalar(T.O[:, 512 * to + b:512 * (to + n):4], sc(T.BI, t, n), tab[:, b:b + 1], None, Op.is_equal).then_inc(s_o, 1)
+            V.tensor_scalar(T.O[:, 512 * to + b:512 * (to + 1):4], sc(T.BI, t), num[:, at + b:at + b + 1], None,
+                            Op.is_equal).then_inc(s_o, 1)
+
+    def pack_o(t, s_o, s_q):
         V.wait_ge(s_o, 4)
-        V.quantize_mx(sc(T.OC, to, n), sc(T.OS, to, n), T.O[:, 512 * to:512 * (to + n)]).then_inc(s_q, 1)
-        return s_q
+        V.quantize_mx(sc(T.OC, t), sc(T.OS, t), T.O[:, 512 * t:512 * (t + 1)]).then_inc(s_q, 1)
 
-    def make_o(t, n):
-        js = R["order"][t:t + n]
-        waits = []
-        if get in js:
-            waits.append((T.sem.oa, 2 * len(off)))
-            if n > 1:
-                t, n, js = (t + 1, n - 1, js[1:]) if js[0] == get else (t, n - 1, js[:-1])
-            else:
-                n = 0
-        if n:
-            for j in js:
-                V.wait_ge(T.sem["id%d" % j], id_count(j))
-            spread(t, n, T.LAND, 4 * t)
-            waits.append((ones(t, t, n, T.VT), 1))
-        return waits
-
-    bank = [0]
-    busy = {}
-
-    def mm_z(t, n, waits):
-        s_c = ev()
-        mine = "v%d" % (cnt[0] - 1)
-        res = []
-        for sem, val in waits:
-            P.wait_ge(sem, val)
-        seen = []
-        for f in range(4):
-            k = bank[0] % NBANK
-            bank[0] += 1
-            if k in busy and busy[k] not in seen:
-                P.wait_ge(T.sem[busy[k]], 4)
-                seen.append(busy[k])
-            busy[k] = mine
-            s_z = ev()
-            P.matmul_mx(T.ZP[:, 512 * k:512 * k + NC * n], sc(T.TC, f), sc(T.TS, f), sc(T.OC, t, n), sc(T.OS, t, n), True, True).then_inc(s_z, 1)
-            res.append((k, s_z))
-        return res, s_c
-
-    def make_e(t, n, z, on_v):
-        res, s_c = z
+    def give_tiles():
         s_q = ev()
-        for f, (k, s_z) in enumerate(res):
-            src = T.ZP[:, 512 * k:512 * k + NC * n]
-            out = T.ET[:, 512 * t + f:512 * (t + n):4]
-            if f in on_v:
-                V.wait_ge(s_z, 1)
-                V.tensor_copy(out, src).then_inc(s_c, 1)
+        s_os = [ev() for _ in give]
+        for i, s_o in enumerate(s_os):
+            compare(NR + i, 0, T.VP, 4 * i, s_o)
+        for i, s_o in enumerate(s_os):
+            pack_o(NR + i, s_o, s_q)
+        ways = [(R["h0"], up, NR), (R["h1"], off, NR + 1)][:len(give)]
+        g.wait_ge(s_q, len(give))
+        return (send(g, T, topo, core, [(h, sc(T.OS, t), sc(T.HS, 0), T.sem.hs0, es) for h, es, t in ways])
+                + send(g, T, topo, core, [(h, cd(T.OC, t), cd(T.HC, 0), T.sem.hc0, es) for h, es, t in ways]))
+
+    banks = {}
+
+    def z_of(t, f):
+        return T.ZP[:, 512 * (banks[t] + f):512 * (banks[t] + f) + NC]
+
+    def products(t):
+        if R["order"][t] == get:
+            P.wait_ge(T.sem.oa, 2 * len(off))
+        else:
+            P.wait_ge(T.sem["o%d" % t], 1)
+        n = len(banks)
+        if n >= 2:
+            P.wait_ge(T.sem["c%d" % list(banks)[n - 2]], 4)
+        banks[t] = n % 2 * 4
+        for f in range(4):
+            P.matmul_mx(z_of(t, f), sc(T.TC, f), sc(T.TS, f), sc(T.OC, t), sc(T.OS, t), True, True).then_inc(T.sem["z%d" % (4 * t + f)], 1)
+
+    def copies(E, t, fs):
+        for f in fs:
+            out = T.ET[:, 512 * t + f:512 * (t + 1):4]
+            E.wait_ge(T.sem["z%d" % (4 * t + f)], 1)
+            if E is V:
+                V.tensor_copy(out, z_of(t, f)).then_inc(T.sem["c%d" % t], 1)
             else:
-                S.wait_ge(s_z, 1)
-                S.activation(out, src, Act.Copy).then_inc(s_c, 1)
-        V.wait_ge(s_c, 4)
-        V.quantize_mx(sc(T.EC, t, n), sc(T.ES, t, n), T.ET[:, 512 * t:512 * (t + n)]).then_inc(s_q, 1)
-        return s_q
+                S.activation(out, z_of(t, f), Act.Copy).then_inc(T.sem["c%d" % t], 1)
 
-    def ship(s_q, items):
-        g.wait_ge(s_q, 1)
-        a = send(g, T, topo, core, [(d, cd(T.EC, t), cd(bc, at), s1, es) for d, t, bc, bs, at, s1, s2, es in items])
-        return a + send(g, T, topo, core, [(d, sc(T.ES, t), sc(bs, at), s2, es) for d, t, bc, bs, at, s1, s2, es in items])
+    def pack_e(t):
+        V.wait_ge(T.sem["c%d" % t], 4)
+        V.quantize_mx(sc(T.EC, t), sc(T.ES, t), T.ET[:, 512 * t:512 * (t + 1)]).then_inc(T.sem["q%d" % t], 1)
 
-    def via(h, t, slot, es):
-        return (R[h], t, T.HC, T.HS, slot, T.sem["hc%d" % slot], T.sem["hs%d" % slot], es)
+    def ship(t):
+        (h, es), = [(h, es) for k, h, es in R["ways"] if k == t]
+        g.wait_ge(T.sem["q%d" % t], 1)
+        if h == "-":
+            d, lc, ls, s1, s2 = cores[R["order"][t]], cd(T.LC, r), sc(T.LS, r), T.sem["ee%d" % r], T.sem["ee%d" % r]
+        else:
+            d, lc, ls, s1, s2 = R[h], cd(T.HC, t), sc(T.HS, t), T.sem["hc%d" % t], T.sem["hs%d" % t]
+        return send(g, T, topo, core, [(d, sc(T.ES, t), ls, s2, es)]) + send(g, T, topo, core, [(d, cd(T.EC, t), lc, s1, es)])
 
-    if give is not None:
-        spread(0, 1, T.MSG, 0)
-        s_g = ones(6, 0, 1, T.VP)
-        g.wait_ge(s_g, 1)
-        loc += send(g, T, topo, core, [(R["h1"], cd(T.OC, 6), cd(T.HC, 3), T.sem.hc3, up)])
-        loc += send(g, T, topo, core, [(R["h1"], sc(T.OS, 6), sc(T.HS, 3), T.sem.hs3, up)])
     s_tq, s_wq = ev(), ev()
-    V.wait_ge(s_tab, 16)
-    V.quantize_mx(T.TC[:], T.TS[:], T.TAB[:]).then_inc(s_tq, 1)
-    P.wait_ge(s_tq, 1)
-
-    m = len(near)
-    t = 1 + m
-    if big:
-        z = mm_z(1, 2, make_o(1, 2))
-        zx = mm_z(t, 2, make_o(t, 2))
-        sq = make_e(1, 2, z, ())
-        loc += ship(sq, [via("h1", 1, 0, up), via("h0", 2, 0, off)])
-        z = mm_z(3, 1, make_o(3, 1))
-        sq = make_e(t, 2, zx, (1, 3))
-        loc += ship(sq, [via("h0", t, 1, up), via("h1", t + 1, 1, off)])
-        sq = make_e(3, 1, z, ())
-        sem = T.sem["ee%d" % r]
-        loc += ship(sq, [(cores[near[2]], 3, T.LC, T.LS, r, sem, sem, off)])
-    else:
-        z = mm_z(1, m, make_o(1, m))
-        sq = make_e(1, m, z, (0, 2))
-        loc += ship(sq, [via("h1", 1, 0, up)])
-        z = mm_z(t, 2, make_o(t, 2))
-        z2 = mm_z(t + 2, 2, make_o(t + 2, 2))
-        sq = make_e(t, 2, z, (3,))
-        loc += ship(sq, [via("h0", t, 1, up), via("h1", t + 1, 1, off)])
-        sq = make_e(t + 2, 2, z2, (1, 3))
-        loc += ship(sq, [via("h0", t + 2, 2, up), via("h1", t + 3, 2, off)])
-
-    if give is None:
-        spread(0, 1, T.MSG, 0)
-    s_own = ones(0, 0, 1, T.VT)
-    V.wait_ge(s_w, 16)
-    V.quantize_mx(T.WC[:], T.WS[:], T.WB[:]).then_inc(s_wq, 1)
-    z = mm_z(0, 1, [(s_own, 1)])
-    s_e0 = make_e(0, 1, z, (0, 2))
+    for w in R["steps"]:
+        a = [int(x) for x in w[1:]] if w[0] != "ship" else [int(w[1])]
+        if w[0] == "own":
+            spread(0, 1, T.MSG, 0)
+        elif w[0] == "give":
+            if give:
+                loc += give_tiles()
+        elif w[0] == "tab":
+            V.wait_ge(s_tab, 16)
+            V.quantize_mx(T.TC[:], T.TS[:], T.TAB[:]).then_inc(s_tq, 1)
+            P.wait_ge(s_tq, 1)
+        elif w[0] == "w":
+            V.wait_ge(s_w, 16)
+            V.quantize_mx(T.WC[:], T.WS[:], T.WB[:]).then_inc(s_wq, 1)
+        elif w[0] == "come":
+            come(a[0], a[1])
+        elif w[0] == "k":
+            compare(a[0], a[0], T.VT, 0, T.sem["k%d" % a[0]])
+        elif w[0] == "o":
+            pack_o(a[0], T.sem["k%d" % a[0]], T.sem["o%d" % a[0]])
+        elif w[0] == "z":
+            products(a[0])
+        elif w[0] == "v":
+            copies(V, a[0], a[1:])
+        elif w[0] == "s":
+            copies(S, a[0], a[1:])
+        elif w[0] == "e":
+            pack_e(a[0])
+        else:
+            loc += ship(a[0])
 
     s_y, s_ys, s_st = ev(), ev(), ev()
-    k = bank[0] % NBANK
-    yp = T.ZP[:, 512 * k:512 * k + NC]
+    t = list(banks)[-2]
+    yp = z_of(t, 0)
+    P.wait_ge(T.sem["c%d" % t], 4)
     P.wait_ge(s_wq, 1)
-    P.wait_ge(T.sem[busy[k]], 4)
-    P.wait_ge(s_e0, 1)
+    P.wait_ge(T.sem.q0, 1)
     P.matmul_mx(yp, T.WC[:], T.WS[:], sc(T.EC, 0), sc(T.ES, 0), True, False)
     order = R["order"][1:]
     for i, j in enumerate(order):

import math
from concourse.bass import DstId, RemoteDMATransfer
from concourse.mybir import dt, AluOpType, ActivationFunctionType

Op = AluOpType
Act = ActivationFunctionType
NR = 6
NC = 128
LN2 = math.log(2.0)

STEPS = {
    "big": ["own", "give", "tab", "come 1 3", "k 1", "o 1", "k 2", "z 1", "k 3", "z 2", "o 2", "come 5 1", "s 1 0 1 2 3",
            "ship 1 h1 u", "e 1", "v 2 0 1 2", "k 5", "o 3", "o 5", "z 4", "e 2", "z 5", "z 3", "ship 2 h0 a", "w", "e 4", "e 5",
            "s 2 3", "ship 4 h0 a", "s 4 0 1 2 3", "s 5 0 1 2 3", "ship 5 h1 a", "k 0", "o 0", "z 0", "e 3", "v 0 0 1 2 3", "e 0",
            "ship 3 - o", "s 3 0 1 2 3"],
    "small": ["own", "give", "come 1 1", "tab", "k 1", "z 1", "z 2", "o 1", "come 3 3", "z 3", "s 1 0 1 2 3", "k 3", "z 4",
              "s 2 0 1 2 3", "e 1", "o 3", "ship 1 h0 a", "k 4", "e 2", "o 4", "s 3 0 1 2 3", "k 5", "o 5", "ship 2 h0 a", "e 3",
              "z 5", "z 0", "v 4 1", "ship 3 h1 a", "s 4 0 2 3", "k 0", "ship 4 h0 a", "e 4", "ship 5 h1 a", "o 0",
              "s 5 0 1 2 3", "w", "e 5", "s 0 0 1 2 3", "e 0"],
}

SCRATCH = {
    "TG": ("sbuf", [128, 384], "bfloat16"),
    "TGT": ("sbuf", [128, 384], "bfloat16"),
    "TAB": ("sbuf", [128, 2048], "bfloat16"),
    "WB": ("sbuf", [128, 512], "bfloat16"),
    "TC": ("sbuf", [128, 512], "float8_e4m3fn_x4"),
    "TS": ("sbuf", [128, 512], "uint8"),
    "WC": ("sbuf", [128, 128], "float8_e4m3fn_x4"),
    "WS": ("sbuf", [128, 128], "uint8"),
    "IOT": ("sbuf", [128, 1], "bfloat16"),
    "C4": ("sbuf", [128, 4], "bfloat16"),
    "KC": ("sbuf", [128, 1], "float32"),
    "KR": ("sbuf", [128, 1], "float32"),
    "VT": ("sbuf", [128, 4], "bfloat16"),
    "VP": ("sbuf", [128, 8], "bfloat16"),
    "E1": ("sbuf", [128, 4], "bfloat16"),
    "E2": ("sbuf", [128, 4], "bfloat16"),
    "P1": ("sbuf", [128, 4], "bfloat16"),
    "X": ("sbuf", [128, 4], "bfloat16"),
    "MSG": ("sbuf", [128, 4], "bfloat16"),
    "LAND": ("sbuf", [128, 4 * NR], "bfloat16"),
    "LANDH": ("sbuf", [128, 4], "bfloat16"),
    "M0": ("sbuf", [128, 3 * NC], "bfloat16"),
    "D1": ("sbuf", [128, NR * NC], "bfloat16"),
    "XB": ("sbuf", [128, NR * NC], "bfloat16"),
    "BI": ("sbuf", [128, NR * NC], "bfloat16"),
    "O": ("sbuf", [128, 8 * 512], "bfloat16"),
    "OC": ("sbuf", [128, 8 * NC], "float8_e4m3fn_x4"),
    "OS": ("sbuf", [128, 8 * NC], "uint8"),
    "ET": ("sbuf", [128, NR * 512], "bfloat16"),
    "EC": ("sbuf", [128, NR * NC], "float8_e4m3fn_x4"),
    "ES": ("sbuf", [128, NR * NC], "uint8"),
    "LC": ("sbuf", [128, NR * NC], "float8_e4m3fn_x4"),
    "LS": ("sbuf", [128, NR * NC], "uint8"),
    "HC": ("sbuf", [128, NR * NC], "float8_e4m3fn_x4"),
    "HS": ("sbuf", [128, NR * NC], "uint8"),
    "YS": ("sbuf", [128, NC], "float32"),
    "ZP": ("psum", [128, 512 * 8], "float32"),
}
NEV = 44
SEMAPHORES = (["v%d" % i for i in range(NEV)]
              + ["%s%d" % (k, i) for k in ("id", "ee", "hc", "hs", "k", "o", "c", "q") for i in range(NR)]
              + ["z%d" % i for i in range(4 * NR)] + ["idh", "oa", "loc"])


def lanes(mask):
    return [e for e in range(mask.bit_length()) if (mask >> e) & 1]


def engine_mask(es):
    return sum(1 << e for e in es)


def split(es, k):
    n = len(es)
    if k == 1:
        return [es]
    if k == 2:
        return [es[:n // 2], es[n // 2:]]
    q = [es[n // 4 * i:n // 4 * (i + 1)] for i in range(4)]
    return [q[0], q[1], q[2] + q[3]] if k == 3 else q


def road(r, T, topo):
    cores = T.cores
    me = cores[r]
    group = [j for j in range(NR) if j == r or topo.same_plane(me, cores[j])]
    far = [j for j in range(NR) if j not in group]
    m = len(group)
    idx = group.index(r)
    near = [group[(idx + 1 + i) % m] for i in range(m - 1)]
    chip = [c for c in range(max(0, me - 8), me + 9) if topo.host(c) == topo.host(me) and topo.chip(c) == topo.chip(me) and c != me]
    port = [c for c in chip if all(topo.may_write(c, cores[j]) for j in far)]
    h0 = [c for c in port if topo.die(c) == topo.die(me)][0]
    h1 = [c for c in port if topo.die(c) != topo.die(me)][0]
    half = len(far) // 2
    a, b = far[:half], far[half:]
    if idx % 2:
        a, b = b, a
    on = lanes(topo.mask(me, h0))
    off = lanes(topo.mask(me, cores[near[0]]))
    up = [e for e in on if e not in off]
    return {"me": me, "far": far, "near": near, "h0": h0, "h1": h1, "pairs": list(zip(a, b))[::-1], "off": off, "up": up,
            "big": len(near) > 1}


def plan(T, topo):
    roads = [road(j, T, topo) for j in range(NR)]
    for R in roads:
        if not R["big"]:
            R["get"] = R["pairs"][0][0]
            R["give"] = [pr[0] for pr in R["pairs"]]
    for j, R in enumerate(roads):
        if R["big"]:
            R["get"] = [k for k in R["far"] if j in roads[k]["give"]][0]
            R["give"] = [k for k in R["far"] if roads[k]["get"] == j]
            R["pairs"] = [(R["get"], [k for k in R["far"] if k != R["get"]][0])]
    for j, R in enumerate(roads):
        rel = [x for x in R["far"] if x not in R["give"]]
        R["relay"] = {"h0": rel[:1], "h1": rel[1:]}
        R["made"] = {"h0": R["give"][:1], "h1": R["give"][1:]}
        R["order"] = [j] + R["near"] + [x for pr in R["pairs"] for x in pr]
        R["tile"] = {x: t for t, x in enumerate(R["order"])}
        R["steps"] = [w.split() for w in STEPS["big" if R["big"] else "small"]]
        R["ways"] = []
        for w in R["steps"]:
            if w[0] == "ship":
                R["ways"].append((int(w[1]), w[2], {"u": R["up"], "o": R["off"], "a": R["off"] + R["up"]}[w[3]]))
    return roads


def send(g, T, topo, src, items):
    tr = []
    n = 0
    for d, s, o, sem, es in items:
        rid, pid = topo.addr(d, src)
        tr.append(RemoteDMATransfer(dst_ids=[DstId(rid=rid, pnc=pid)], dma_engine_mask=engine_mask(es), remote_sem=sem, src=s, dst=o))
        n += len(es)
    g.remote_dma_fused(tr, local_sem=T.sem.loc)
    return n


def cd(t, i):
    return t[:, NC * i:NC * (i + 1)].bitcast(dt.uint8)


def sc(t, i, n=1):
    return t[:, NC * i:NC * (i + n)]


def four(t, i):
    return t[:, 4 * i:4 * i + 4]


def to_helpers(R):
    hs = [h for h in ("h0", "h1") if R["relay"][h]]
    return dict(zip(hs, split(R["up"], len(hs))))


def helper_program(g, core, r, roads, T, topo):
    cores = T.cores
    R = roads[r]
    me = "h0" if core == R["h0"] else "h1"
    loc = 0
    for j in R["relay"][me]:
        g.wait_ge(T.sem.idh, len(to_helpers(R)[me]))
        loc += send(g, T, topo, core, [(cores[j], T.LANDH[:], four(T.LAND, roads[j]["tile"][r]), T.sem["id%d" % r], R["off"])])
    todo = [(0, R["up" if me == "h0" else "off"], j, (T.OC, T.OS, roads[j]["tile"][r]), T.sem.oa) for j in R["made"][me]]
    todo += [(t, es, R["order"][t], (T.LC, T.LS, r), T.sem["ee%d" % r]) for t, h, es in R["ways"] if h == me]
    for t, es, j, (bc, bs, at), sem in todo:
        g.wait_ge(T.sem["hs%d" % t], len(es))
        loc += send(g, T, topo, core, [(cores[j], sc(T.HS, t), sc(bs, at), sem, R["off"])])
        g.wait_ge(T.sem["hc%d" % t], len(es))
        loc += send(g, T, topo, core, [(cores[j], cd(T.HC, t), cd(bc, at), sem, R["off"])])
    g.wait_ge(T.sem.loc, loc)


def rank_core(g, core, r, roads, T, topo):
    cores = T.cores
    R = roads[r]
    V, S, P = g.vector, g.scalar, g.tensor
    cnt = [0]

    def ev():
        cnt[0] += 1
        return T.sem["v%d" % (cnt[0] - 1)]

    near, give, get = R["near"], R["give"], R["get"]
    off, up = R["off"], R["up"]

    def id_count(j):
        Q = roads[j]
        if r in Q["near"]:
            return len(split(Q["off"], len(Q["near"]))[Q["near"].index(r)])
        return len(Q["off"])

    s_tg, s_tab, s_w = ev(), ev(), ev()
    g.sync.dma_start(T.TG[:], T.tg[:]).then_inc(s_tg, 16)
    g.sync.dma_start(T.TAB[:], T.tab[:]).then_inc(s_tab, 16)
    g.sync.dma_start(T.WB[:], T.w[:]).then_inc(s_w, 16)

    s_io, s_kc, s_kr, s_m, s_m2, s_c4 = ev(), ev(), ev(), ev(), ev(), ev()
    g.iota(T.IOT[:], [[1, 1]], 1, 1, allow_small_or_imprecise_dtypes=True).then_inc(s_io, 1)
    V.memset(T.KC[:], float(r)).then_inc(s_kc, 1)
    S.wait_ge(s_kc, 1)
    S.activation(T.KR[:], T.KC[:], Act.Exp, bias=-95.0 * LN2, scale=32.0 * LN2).then_inc(s_kr, 1)
    V.memset(T.M0[:], 1.0).then_inc(s_m, 1)
    V.memset(T.D1[:], 0.0).then_inc(s_m, 1)
    V.wait_ge(s_io, 1)
    for b in range(4):
        V.tensor_scalar(T.C4[:, b:b + 1], T.IOT[:], float(2.0 ** (8 * b)), None, Op.mult).then_inc(s_c4, 1)
    V.wait_ge(s_m, 2)
    V.memset(T.M0[:, 0:3 * NC:32], 0.0).then_inc(s_m2, 1)

    s_tb, s_t, s_tp, s_e2, s_e1, s_p, s_x, s_msg = ev(), ev(), ev(), ev(), ev(), ev(), ev(), ev()
    V.wait_ge(s_tg, 16)
    V.transpose(T.TGT[:, 256:384], T.TG[:, 256:384]).then_inc(s_tb, 1)
    V.transpose(T.TGT[:, 128:256], T.TG[:, 128:256]).then_inc(s_tp, 1)
    V.transpose(T.TGT[:, 0:128], T.TG[:, 0:128]).then_inc(s_t, 1)
    S.wait_ge(s_tb, 1)
    S.activation(T.E2[:], T.TGT[:, 256:384:32], Act.Exp, scale=8.0 * LN2).then_inc(s_e2, 1)
    S.wait_ge(s_t, 1)
    S.activation(T.E1[:], T.TGT[:, 0:128:32], Act.Exp, bias=-95.0 * LN2, scale=32.0 * LN2).then_inc(s_e1, 1)
    V.wait_ge(s_tp, 1)
    V.tensor_scalar(T.P1[:], T.TGT[:, 128:256:32], 1.0, None, Op.add).then_inc(s_p, 1)
    V.wait_ge(s_p, 1)
    V.wait_ge(s_e2, 1)
    V.tensor_tensor(T.X[:], T.P1[:], T.E2[:], Op.mult).then_inc(s_x, 1)
    V.wait_ge(s_x, 1)
    V.wait_ge(s_e1, 1)
    V.tensor_tensor(T.MSG[:], T.X[:], T.E1[:], Op.mult).then_inc(s_msg, 1)

    loc = 0
    g.wait_ge(s_msg, 1)
    loc += send(g, T, topo, core, [(R[h], T.MSG[:], T.LANDH[:], T.sem.idh, es) for h, es in to_helpers(R).items()])
    parts = split(off, len(near))
    loc += send(g, T, topo, core, [(cores[j], T.MSG[:], four(T.LAND, roads[j]["tile"][r]), T.sem["id%d" % r], parts[i])
                                   for i, j in enumerate(near)])

    s_vt = ev()
    V.wait_ge(s_c4, 4)
    V.wait_ge(s_kr, 1)
    V.wait_ge(s_m2, 1)
    for i, k in enumerate(give):
        V.tensor_scalar(four(T.VP, i), T.C4[:], T.KR[:], float(2.0 ** (32 * (k - r))), Op.mult, Op.mult).then_inc(s_vt, 1)
    V.tensor_scalar(T.VT[:], T.C4[:], T.KR[:], None, Op.mult).then_inc(s_vt, 1)
    V.wait_ge(s_msg, 1)
    V.wait_ge(s_vt, 1 + len(give))

    def spread(t, n, buf, c0):
        s_d, s_s, s_b = ev(), ev(), ev()
        V.tensor_copy(T.D1[:, NC * t:NC * (t + n):32], buf[:, c0:c0 + 4 * n]).then_inc(s_d, 1)
        V.wait_ge(s_d, 1)
        V.tensor_tensor_scan(sc(T.XB, t, n), sc(T.M0, 0, n), sc(T.D1, t, n), 0.0, Op.mult, Op.add).then_inc(s_s, 1)
        V.wait_ge(s_s, 1)
        V.transpose(sc(T.BI, t, n), sc(T.XB, t, n)).then_inc(s_b, 1)
        V.wait_ge(s_b, 1)

    def come(t, n):
        for j in R["order"][t:t + n]:
            V.wait_ge(T.sem["id%d" % j], id_count(j))
        spread(t, n, T.LAND, 4 * t)

    def compare(to, t, num, at, s_o):
        for b in range(4):
            V.tensor_scalar(T.O[:, 512 * to + b:512 * (to + 1):4], sc(T.BI, t), num[:, at + b:at + b + 1], None,
                            Op.is_equal).then_inc(s_o, 1)

    def pack_o(t, s_o, s_q):
        V.wait_ge(s_o, 4)
        V.quantize_mx(sc(T.OC, t), sc(T.OS, t), T.O[:, 512 * t:512 * (t + 1)]).then_inc(s_q, 1)

    def give_tiles():
        s_q = ev()
        s_os = [ev() for _ in give]
        for i, s_o in enumerate(s_os):
            compare(NR + i, 0, T.VP, 4 * i, s_o)
        for i, s_o in enumerate(s_os):
            pack_o(NR + i, s_o, s_q)
        ways = [(R["h0"], up, NR), (R["h1"], off, NR + 1)][:len(give)]
        g.wait_ge(s_q, len(give))
        return (send(g, T, topo, core, [(h, sc(T.OS, t), sc(T.HS, 0), T.sem.hs0, es) for h, es, t in ways])
                + send(g, T, topo, core, [(h, cd(T.OC, t), cd(T.HC, 0), T.sem.hc0, es) for h, es, t in ways]))

    banks = {}

    def z_of(t, f):
        return T.ZP[:, 512 * (banks[t] + f):512 * (banks[t] + f) + NC]

    def products(t):
        if R["order"][t] == get:
            P.wait_ge(T.sem.oa, 2 * len(off))
        else:
            P.wait_ge(T.sem["o%d" % t], 1)
        n = len(banks)
        if n >= 2:
            P.wait_ge(T.sem["c%d" % list(banks)[n - 2]], 4)
        banks[t] = n % 2 * 4
        for f in range(4):
            P.matmul_mx(z_of(t, f), sc(T.TC, f), sc(T.TS, f), sc(T.OC, t), sc(T.OS, t), True, True).then_inc(T.sem["z%d" % (4 * t + f)], 1)

    def copies(E, t, fs):
        for f in fs:
            out = T.ET[:, 512 * t + f:512 * (t + 1):4]
            E.wait_ge(T.sem["z%d" % (4 * t + f)], 1)
            if E is V:
                V.tensor_copy(out, z_of(t, f)).then_inc(T.sem["c%d" % t], 1)
            else:
                S.activation(out, z_of(t, f), Act.Copy).then_inc(T.sem["c%d" % t], 1)

    def pack_e(t):
        V.wait_ge(T.sem["c%d" % t], 4)
        V.quantize_mx(sc(T.EC, t), sc(T.ES, t), T.ET[:, 512 * t:512 * (t + 1)]).then_inc(T.sem["q%d" % t], 1)

    def ship(t):
        (h, es), = [(h, es) for k, h, es in R["ways"] if k == t]
        g.wait_ge(T.sem["q%d" % t], 1)
        if h == "-":
            d, lc, ls, s1, s2 = cores[R["order"][t]], cd(T.LC, r), sc(T.LS, r), T.sem["ee%d" % r], T.sem["ee%d" % r]
        else:
            d, lc, ls, s1, s2 = R[h], cd(T.HC, t), sc(T.HS, t), T.sem["hc%d" % t], T.sem["hs%d" % t]
        return send(g, T, topo, core, [(d, sc(T.ES, t), ls, s2, es)]) + send(g, T, topo, core, [(d, cd(T.EC, t), lc, s1, es)])

    s_tq, s_wq = ev(), ev()
    for w in R["steps"]:
        a = [int(x) for x in w[1:]] if w[0] != "ship" else [int(w[1])]
        if w[0] == "own":
            spread(0, 1, T.MSG, 0)
        elif w[0] == "give":
            if give:
                loc += give_tiles()
        elif w[0] == "tab":
            V.wait_ge(s_tab, 16)
            V.quantize_mx(T.TC[:], T.TS[:], T.TAB[:]).then_inc(s_tq, 1)
            P.wait_ge(s_tq, 1)
        elif w[0] == "w":
            V.wait_ge(s_w, 16)
            V.quantize_mx(T.WC[:], T.WS[:], T.WB[:]).then_inc(s_wq, 1)
        elif w[0] == "come":
            come(a[0], a[1])
        elif w[0] == "k":
            compare(a[0], a[0], T.VT, 0, T.sem["k%d" % a[0]])
        elif w[0] == "o":
            pack_o(a[0], T.sem["k%d" % a[0]], T.sem["o%d" % a[0]])
        elif w[0] == "z":
            products(a[0])
        elif w[0] == "v":
            copies(V, a[0], a[1:])
        elif w[0] == "s":
            copies(S, a[0], a[1:])
        elif w[0] == "e":
            pack_e(a[0])
        else:
            loc += ship(a[0])

    s_y, s_ys, s_st = ev(), ev(), ev()
    t = list(banks)[-2]
    yp = z_of(t, 0)
    P.wait_ge(T.sem["c%d" % t], 4)
    P.wait_ge(s_wq, 1)
    P.wait_ge(T.sem.q0, 1)
    P.matmul_mx(yp, T.WC[:], T.WS[:], sc(T.EC, 0), sc(T.ES, 0), True, False)
    order = R["order"][1:]
    for i, j in enumerate(order):
        P.wait_ge(T.sem["ee%d" % j], 2 * len(off))
        last = i == len(order) - 1
        c = P.matmul_mx(yp, T.WC[:], T.WS[:], sc(T.LC, j), sc(T.LS, j), False, last)
        if last:
            c.then_inc(s_y, 1)
    V.wait_ge(s_y, 1)
    V.tensor_copy(T.YS[:], yp).then_inc(s_ys, 1)
    g.sync.wait_ge(s_ys, 1)
    g.sync.dma_start(T.y[:], T.YS[:]).then_inc(s_st, 16)
    g.sync.wait_ge(s_st, 16)
    g.wait_ge(T.sem.loc, loc)


def rank_program(g, core, T, topo):
    roads = plan(T, topo)
    r = T.rank_of(core)
    if r is not None:
        rank_core(g, core, r, roads, T, topo)
        return
    for r in range(NR):
        if core in (roads[r]["h0"], roads[r]["h1"]):
            helper_program(g, core, r, roads, T, topo)
